import numpy as np
import ml_dtypes


def mxq(x, axis, fmt="e4m3"):
    dtype, down = {"e4m3": (ml_dtypes.float8_e4m3fn, 7), "e5m2": (ml_dtypes.float8_e5m2, 14)}[fmt]
    v = np.moveaxis(np.asarray(x, np.float32).astype(ml_dtypes.bfloat16).astype(np.float64), axis, -1)
    blocks = v.reshape(v.shape[:-1] + (-1, 32))
    amax = np.abs(blocks).max(-1, keepdims=True)
    byte = np.maximum(np.where(amax > 0, np.frexp(amax)[1] - 1 + 127, 0) - down, 1)
    scale = np.exp2(byte - 127.0)
    codes = (blocks / scale).astype(np.float32).astype(dtype).astype(np.float64)
    return np.moveaxis((codes * scale).reshape(v.shape), -1, axis)


WIDE = False


def mx_kscale(k):
    if not WIDE:
        return np.ones(k)
    levels = np.array([10, -10, 5, -5, 0])
    if k % 512:
        return np.exp2(np.random.permutation(np.resize(levels, k // 32))).repeat(32)
    a = np.empty((k // 512, 16))
    for p in range(k // 512):
        a[p, :8] = np.random.permutation(np.resize(levels, 8))
        for g in range(8):
            far = levels[np.abs(levels - a[p, g]) >= 10]
            a[p, g + 8] = far[np.random.randint(len(far))]
    return np.exp2(a.ravel()).repeat(32)


def f64(x):
    return np.asarray(x).astype(np.float64)


def striped(idx):
    return np.tile(idx.reshape(-1, 16).T, (8, 1)).astype(np.uint16)


def unstriped(offs):
    return offs[:16].T.reshape(-1).astype(np.int64)


K, T, D, S, V, N = 512, 1024, 8, 4096, 512, 512


def setup_inputs():
    n = np.random.standard_normal
    s = mx_kscale(K)[:, None]
    return {
        "xT": (n((K, T)) * s).astype(np.float32),
        "w": (n((K, N)) / np.sqrt(K) / s).astype(np.float32),
        "b": (0.3 * n((N, 1))).astype(np.float32),
        "gate": np.tile(np.random.uniform(0.2, 1.0, (D, 1, V)) / np.sqrt(D), (1, N, 1)).astype(np.float32),
        "pos1": striped(np.random.permutation(T)[:V]),
        "pos2": striped(np.random.permutation(T)[:V]),
        "pos3": striped(np.random.permutation(T)[:V]),
        "pos4": striped(np.random.permutation(T)[:V]),
        "pos5": striped(np.random.permutation(T)[:V]),
        "pos6": striped(np.random.permutation(T)[:V]),
        "pos7": striped(np.random.permutation(T)[:V]),
        "pos8": striped(np.random.permutation(T)[:V]),
    }


def reference(xT, w, b, gate, pos1, pos2, pos3, pos4, pos5, pos6, pos7, pos8):
    y = mxq(f64(w), 0, "e4m3").T @ mxq(f64(xT), 0, "e4m3")
    y = y + f64(b)
    return sum(f64(gate[d]) * y[:, unstriped(p)] for d, p in enumerate((pos1, pos2, pos3, pos4, pos5, pos6, pos7, pos8)))

@@ -1,0 +1,173 @@
+from contextlib import ExitStack
+
+import concourse.mybir as mybir
+from concourse.masks import make_identity
+
+K, T, D, V, N = 512, 1024, 8, 512, 512
+P = 128
+PACK = 4
+BLOCKS = N // P
+CHUNKS = ((0, 512), (512, 256), (768, 256))
+
+F32 = mybir.dt.float32
+BF16 = mybir.dt.bfloat16
+U32 = mybir.dt.uint32
+U16 = mybir.dt.uint16
+U8 = mybir.dt.uint8
+FP8X4 = mybir.dt.float8_e4m3fn_x4
+MULT = mybir.AluOpType.mult
+ADD = mybir.AluOpType.add
+IDENTITY = mybir.ActivationFunctionType.Identity
+
+FLOPS = 2 * K * N * T + 2 * D * N * V
+
+
+def tile_picked_agg_lin_bias_sub_l_kernel(
+    tc, xT, w, b, gate, pos1, pos2, pos3, pos4, pos5, pos6, pos7, pos8, out
+):
+    nc = tc.nc
+    lists = (pos1, pos2, pos3, pos4, pos5, pos6, pos7, pos8)
+    with ExitStack() as ctx:
+        keep = ctx.enter_context(tc.tile_pool(name="keep", bufs=1))
+        ring = ctx.enter_context(tc.tile_pool(name="ring", bufs=6))
+        flip = ctx.enter_context(tc.tile_pool(name="flip", bufs=2))
+        psum = ctx.enter_context(tc.psum_pool(name="psum", bufs=1))
+
+        w_view = w.rearrange("(p j) m -> p j m", j=PACK)
+        x_view = xT.rearrange("(p j) t -> p j t", j=PACK)
+
+        ident = keep.tile([P, P], F32, name="ident")
+        b_rows = keep.tile([P, P], F32, name="b_rows")
+        bias = keep.tile([P, BLOCKS], F32, name="bias")
+        warm = keep.tile([P, 1], F32, name="warm")
+
+        w_raw = [keep.tile([P, PACK, P], F32, name="w_raw%d" % i) for i in range(BLOCKS)]
+        w_bf = [keep.tile([P, P, PACK], BF16, name="w_bf%d" % i, align_bytes=64) for i in range(BLOCKS)]
+        w_codes = [keep.tile([P, P], U32, name="w_codes%d" % i, align_bytes=64) for i in range(BLOCKS)]
+        w_scales = [keep.tile([P, P], U8, name="w_scales%d" % i, align_bytes=64) for i in range(BLOCKS)]
+        x_raw = [keep.tile([P, PACK, n], F32, name="x_raw%d" % c) for c, (t0, n) in enumerate(CHUNKS)]
+        x_bf = [keep.tile([P, n, PACK], BF16, name="x_bf%d" % c, align_bytes=64) for c, (t0, n) in enumerate(CHUNKS)]
+        x_codes = [keep.tile([P, n], U32, name="x_codes%d" % c, align_bytes=64) for c, (t0, n) in enumerate(CHUNKS)]
+        x_scales = [keep.tile([P, n], U8, name="x_scales%d" % c, align_bytes=64) for c, (t0, n) in enumerate(CHUNKS)]
+        pos = [keep.tile([P, V // 16], U16, name="pos_%d" % d) for d in range(D)]
+        gates = [keep.tile([P, D, V], F32, name="gates%d" % i) for i in range(BLOCKS)]
+        y = [keep.tile([P, T], F32, name="y%d" % i) for i in range(BLOCKS)]
+
+        def load_gates(i, d0, d1):
+            nc.sync.dma_start(
+                out=gates[i][:, d0:d1, :],
+                in_=gate[d0:d1, i * P : (i + 1) * P, :].rearrange("d p v -> p d v"),
+            )
+
+        nc.sync.dma_start(out=w_raw[0][:], in_=w_view[:, :, 0:P])
+        for c, (t0, n) in enumerate(CHUNKS):
+            nc.sync.dma_start(out=x_raw[c][:], in_=x_view[:, :, t0 : t0 + n])
+        nc.vector.memset(warm[:], 0.0)
+        nc.scalar.activation(warm[:], warm[:], IDENTITY)
+        nc.gpsimd.memset(b_rows[:], 0.0)
+        nc.scalar.dma_start(out=b_rows[0:BLOCKS, :], in_=b.rearrange("(c p) o -> c (p o)", p=P))
+        make_identity(nc, ident[:])
+        for d in range(D):
+            nc.sync.dma_start(pos[d][:], lists[d])
+            if d < 2:
+                load_gates(0, d, d + 1)
+            elif d % 2 == 1:
+                load_gates(0, d - 1, d + 1)
+            if d == 3:
+                nc.sync.dma_start(out=w_raw[1][:], in_=w_view[:, :, P : 2 * P])
+        for i in range(1, BLOCKS):
+            for d in range(0, D, 2):
+                load_gates(i, d, d + 2)
+                if d == 2 and i + 1 < BLOCKS:
+                    nc.sync.dma_start(out=w_raw[i + 1][:], in_=w_view[:, :, (i + 1) * P : (i + 2) * P])
+
+        def quantize_w(i):
+            nc.vector.quantize_mx(
+                out=w_codes[i][:].bitcast(FP8X4),
+                scales=w_scales[i][:],
+                in_=w_bf[i][:].rearrange("p m j -> p (m j)"),
+            )
+
+        def project(i, c, bank, col):
+            t0, n = CHUNKS[c]
+            nc.tensor.matmul_mx(
+                out=bank[:, col : col + n],
+                lhsT=w_codes[i][:].bitcast(FP8X4),
+                lhsT_scale=w_scales[i][:],
+                rhs=x_codes[c][:].bitcast(FP8X4),
+                rhs_scale=x_scales[c][:],
+                start=True,
+                stop=True,
+            )
+
+        b_bank = psum.tile([P, V], F32, name="back")
+        nc.tensor.transpose(b_bank[:, 0:P], b_rows[:], ident[:])
+        nc.scalar.copy(bias[:], b_bank[:, 0:BLOCKS])
+
+        nc.vector.tensor_copy(out=w_bf[0][:], in_=w_raw[0][:].rearrange("p j m -> p m j"))
+        quantize_w(0)
+        banks = [psum.tile([P, V], F32, name="y_bank%d" % h) for h in range(2)]
+        for c, (t0, n) in enumerate(CHUNKS):
+            cut = n * 5 // 8
+            src = x_raw[c][:].rearrange("p j t -> p t j")
+            nc.vector.tensor_copy(out=x_bf[c][:, 0:cut, :], in_=src[:, 0:cut, :])
+            nc.scalar.copy(x_bf[c][:, cut:n, :], src[:, cut:n, :])
+            nc.vector.quantize_mx(
+                out=x_codes[c][:].bitcast(FP8X4),
+                scales=x_scales[c][:],
+                in_=x_bf[c][:].rearrange("p t j -> p (t j)"),
+            )
+            bank, col = banks[t0 // V], t0 % V
+            project(0, c, bank, col)
+            if c == len(CHUNKS) - 1:
+                nc.vector.tensor_scalar(
+                    out=y[0][:, t0 : t0 + n], in0=bank[:, col : col + n], scalar1=bias[:, 0:1], scalar2=None, op0=ADD
+                )
+            else:
+                nc.scalar.activation(y[0][:, t0 : t0 + n], bank[:, col : col + n], IDENTITY, bias=bias[:, 0:1])
+
+        def prepare_block(i):
+            nc.scalar.copy(w_bf[i][:], w_raw[i][:].rearrange("p j m -> p m j"))
+            quantize_w(i)
+            next_banks = [psum.tile([P, V], F32, name="y_bank%d" % h) for h in range(2)]
+            for c, (t0, n) in enumerate(CHUNKS):
+                project(i, c, next_banks[t0 // V], t0 % V)
+            for h in range(2):
+                nc.scalar.activation(y[i][:, h * V : (h + 1) * V], next_banks[h][:], IDENTITY, bias=bias[:, i : i + 1])
+
+        for i in range(BLOCKS):
+            last_block = i == BLOCKS - 1
+            summed = D - 1 if last_block else D
+            acc = [psum.tile([P, P], F32, name="acc%d" % q) for q in range(V // P)]
+            for d in range(summed):
+                g = ring.tile([P, V], F32, name="g")
+                nc.vector.tensor_tensor(g[:], y[i][:].indirect(pos[d][:]), gates[i][:, d, :], MULT)
+                for q in range(V // P):
+                    nc.tensor.matmul(
+                        acc[q][:], g[:, q * P : (q + 1) * P], ident[:], start=(d == 0), stop=(d == summed - 1), is_transpose=True
+                    )
+                if d == 3 and not last_block:
+                    prepare_block(i + 1)
+            turned = flip.tile([P, V], F32, name="turned")
+            back = psum.tile([P, V], F32, name="back")
+            for q in range(V // P):
+                nc.scalar.copy(turned[:, q * P : (q + 1) * P], acc[q][:])
+                nc.tensor.transpose(back[:, q * P : (q + 1) * P], turned[:, q * P : (q + 1) * P], ident[:])
+            result = flip.tile([P, V], F32, name="result")
+            if not last_block:
+                nc.scalar.copy(result[:], back[:])
+                nc.scalar.dma_start(out=out[i * P : (i + 1) * P, :], in_=result[:])
+            else:
+                half = V // 2
+                tail = [ring.tile([P, half], F32, name="tail%d" % h) for h in range(2)]
+                for h in range(2):
+                    nc.vector.tensor_tensor(
+                        tail[h][:],
+                        y[i][:].indirect(pos[D - 1][:, h * half // 16 : (h + 1) * half // 16]),
+                        gates[i][:, D - 1, h * half : (h + 1) * half],
+                        MULT,
+                    )
+                for h in range(2):
+                    cols = slice(h * half, (h + 1) * half)
+                    nc.vector.tensor_tensor(result[:, cols], back[:, cols], tail[h][:], ADD)
+                    nc.sync.dma_start(out=out[i * P : (i + 1) * P, cols], in_=result[:, cols])

@@ -7,7 +7,9 @@ K, T, D, V, N = 512, 1024, 8, 512, 512
 P = 128
 PACK = 4
 BLOCKS = N // P
-CHUNKS = ((0, 512), (512, 256), (768, 256))
+CHUNK = 256
+CHUNKS = tuple((t0, CHUNK) for t0 in range(0, T, CHUNK))
+TAIL = ((0, 384), (384, 128))
 
 F32 = mybir.dt.float32
 BF16 = mybir.dt.bfloat16
@@ -37,7 +39,6 @@ def tile_picked_agg_lin_bias_sub_l_kernel(
         x_view = xT.rearrange("(p j) t -> p j t", j=PACK)
 
         ident = keep.tile([P, P], F32, name="ident")
-        b_rows = keep.tile([P, P], F32, name="b_rows")
         bias = keep.tile([P, BLOCKS], F32, name="bias")
         warm = keep.tile([P, 1], F32, name="warm")
 
@@ -59,14 +60,13 @@ def tile_picked_agg_lin_bias_sub_l_kernel(
                 in_=gate[d0:d1, i * P : (i + 1) * P, :].rearrange("d p v -> p d v"),
             )
 
+        make_identity(nc, ident[:])
+        nc.vector.memset(warm[:], 0.0)
+        nc.scalar.activation(warm[:], warm[:], IDENTITY)
         nc.sync.dma_start(out=w_raw[0][:], in_=w_view[:, :, 0:P])
         for c, (t0, n) in enumerate(CHUNKS):
             nc.sync.dma_start(out=x_raw[c][:], in_=x_view[:, :, t0 : t0 + n])
-        nc.vector.memset(warm[:], 0.0)
-        nc.scalar.activation(warm[:], warm[:], IDENTITY)
-        nc.gpsimd.memset(b_rows[:], 0.0)
-        nc.scalar.dma_start(out=b_rows[0:BLOCKS, :], in_=b.rearrange("(c p) o -> c (p o)", p=P))
-        make_identity(nc, ident[:])
+        nc.sync.dma_start(out=bias[:], in_=b.rearrange("(c p) o -> p (c o)", p=P))
         for d in range(D):
             nc.sync.dma_start(pos[d][:], lists[d])
             if d < 2:
@@ -100,31 +100,47 @@ def tile_picked_agg_lin_bias_sub_l_kernel(
                 stop=True,
             )
 
-        b_bank = psum.tile([P, V], F32, name="back")
-        nc.tensor.transpose(b_bank[:, 0:P], b_rows[:], ident[:])
-        nc.scalar.copy(bias[:], b_bank[:, 0:BLOCKS])
-
         nc.vector.tensor_copy(out=w_bf[0][:], in_=w_raw[0][:].rearrange("p j m -> p m j"))
         quantize_w(0)
-        banks = [psum.tile([P, V], F32, name="y_bank%d" % h) for h in range(2)]
-        for c, (t0, n) in enumerate(CHUNKS):
-            cut = n * 5 // 8
+
+        def regroup_x(c):
+            n = CHUNKS[c][1]
+            cut = n // 2 if c < len(CHUNKS) - 1 else n * 5 // 8
             src = x_raw[c][:].rearrange("p j t -> p t j")
-            nc.vector.tensor_copy(out=x_bf[c][:, 0:cut, :], in_=src[:, 0:cut, :])
             nc.scalar.copy(x_bf[c][:, cut:n, :], src[:, cut:n, :])
+            nc.vector.tensor_copy(out=x_bf[c][:, 0:cut, :], in_=src[:, 0:cut, :])
+
+        def quantize_x(c):
             nc.vector.quantize_mx(
                 out=x_codes[c][:].bitcast(FP8X4),
                 scales=x_scales[c][:],
                 in_=x_bf[c][:].rearrange("p t j -> p (t j)"),
             )
-            bank, col = banks[t0 // V], t0 % V
-            project(0, c, bank, col)
-            if c == len(CHUNKS) - 1:
-                nc.vector.tensor_scalar(
-                    out=y[0][:, t0 : t0 + n], in0=bank[:, col : col + n], scalar1=bias[:, 0:1], scalar2=None, op0=ADD
-                )
+
+        def add_bias(engine_is_scalar, bank, t0, n):
+            if engine_is_scalar:
+                nc.scalar.activation(y[0][:, t0 : t0 + n], bank[:, 0:n], IDENTITY, bias=bias[:, 0:1])
             else:
-                nc.scalar.activation(y[0][:, t0 : t0 + n], bank[:, col : col + n], IDENTITY, bias=bias[:, 0:1])
+                nc.vector.tensor_scalar(
+                    out=y[0][:, t0 : t0 + n], in0=bank[:, 0:n], scalar1=bias[:, 0:1], scalar2=None, op0=ADD
+                )
+
+        head_banks = [psum.tile([P, V], F32, name=tag) for tag in ("y_bank0", "y_bank1", "y_bank2")]
+        regroup_x(0)
+        regroup_x(1)
+        quantize_x(0)
+        project(0, 0, head_banks[0], 0)
+        regroup_x(2)
+        quantize_x(1)
+        project(0, 1, head_banks[0], CHUNK)
+        regroup_x(3)
+        add_bias(True, head_banks[0], 0, 2 * CHUNK)
+        quantize_x(2)
+        project(0, 2, head_banks[1], 0)
+        quantize_x(3)
+        project(0, 3, head_banks[2], 0)
+        add_bias(False, head_banks[1], 2 * CHUNK, CHUNK)
+        add_bias(False, head_banks[2], 3 * CHUNK, CHUNK)
 
         def prepare_block(i):
             nc.scalar.copy(w_bf[i][:], w_raw[i][:].rearrange("p j m -> p m j"))
@@ -158,16 +174,15 @@ def tile_picked_agg_lin_bias_sub_l_kernel(
                 nc.scalar.copy(result[:], back[:])
                 nc.scalar.dma_start(out=out[i * P : (i + 1) * P, :], in_=result[:])
             else:
-                half = V // 2
-                tail = [ring.tile([P, half], F32, name="tail%d" % h) for h in range(2)]
-                for h in range(2):
+                tail = [ring.tile([P, n], F32, name="tail%d" % h) for h, (v0, n) in enumerate(TAIL)]
+                for h, (v0, n) in enumerate(TAIL):
                     nc.vector.tensor_tensor(
                         tail[h][:],
-                        y[i][:].indirect(pos[D - 1][:, h * half // 16 : (h + 1) * half // 16]),
-                        gates[i][:, D - 1, h * half : (h + 1) * half],
+                        y[i][:].indirect(pos[D - 1][:, v0 // 16 : (v0 + n) // 16]),
+                        gates[i][:, D - 1, v0 : v0 + n],
                         MULT,
                     )
-                for h in range(2):
-                    cols = slice(h * half, (h + 1) * half)
+                for h, (v0, n) in enumerate(TAIL):
+                    cols = slice(v0, v0 + n)
                     nc.vector.tensor_tensor(result[:, cols], back[:, cols], tail[h][:], ADD)
                     nc.sync.dma_start(out=out[i * P : (i + 1) * P, cols], in_=result[:, cols])

@@ -9,6 +9,7 @@ PACK = 4
 BLOCKS = N // P
 CHUNK = 256
 CHUNKS = tuple((t0, CHUNK) for t0 in range(0, T, CHUNK))
+X_LOADS = ((0, 512), (512, 256), (768, 256))
 TAIL = ((0, 384), (384, 128))
 
 F32 = mybir.dt.float32
@@ -46,7 +47,7 @@ def tile_picked_agg_lin_bias_sub_l_kernel(
         w_bf = [keep.tile([P, P, PACK], BF16, name="w_bf%d" % i, align_bytes=64) for i in range(BLOCKS)]
         w_codes = [keep.tile([P, P], U32, name="w_codes%d" % i, align_bytes=64) for i in range(BLOCKS)]
         w_scales = [keep.tile([P, P], U8, name="w_scales%d" % i, align_bytes=64) for i in range(BLOCKS)]
-        x_raw = [keep.tile([P, PACK, n], F32, name="x_raw%d" % c) for c, (t0, n) in enumerate(CHUNKS)]
+        x_raw = [keep.tile([P, PACK, n], F32, name="x_raw%d" % c) for c, (t0, n) in enumerate(X_LOADS)]
         x_bf = [keep.tile([P, n, PACK], BF16, name="x_bf%d" % c, align_bytes=64) for c, (t0, n) in enumerate(CHUNKS)]
         x_codes = [keep.tile([P, n], U32, name="x_codes%d" % c, align_bytes=64) for c, (t0, n) in enumerate(CHUNKS)]
         x_scales = [keep.tile([P, n], U8, name="x_scales%d" % c, align_bytes=64) for c, (t0, n) in enumerate(CHUNKS)]
@@ -64,22 +65,34 @@ def tile_picked_agg_lin_bias_sub_l_kernel(
         nc.vector.memset(warm[:], 0.0)
         nc.scalar.activation(warm[:], warm[:], IDENTITY)
         nc.sync.dma_start(out=w_raw[0][:], in_=w_view[:, :, 0:P])
-        for c, (t0, n) in enumerate(CHUNKS):
+        for c, (t0, n) in enumerate(X_LOADS):
             nc.sync.dma_start(out=x_raw[c][:], in_=x_view[:, :, t0 : t0 + n])
         nc.sync.dma_start(out=bias[:], in_=b.rearrange("(c p) o -> p (c o)", p=P))
-        for d in range(D):
+        def load_list(d):
             nc.sync.dma_start(pos[d][:], lists[d])
-            if d < 2:
-                load_gates(0, d, d + 1)
-            elif d % 2 == 1:
-                load_gates(0, d - 1, d + 1)
-            if d == 3:
-                nc.sync.dma_start(out=w_raw[1][:], in_=w_view[:, :, P : 2 * P])
+
+        def load_w(i):
+            nc.sync.dma_start(out=w_raw[i][:], in_=w_view[:, :, i * P : (i + 1) * P])
+
+        load_list(0)
+        load_gates(0, 0, 1)
+        load_list(1)
+        load_gates(0, 1, 2)
+        load_list(2)
+        load_gates(0, 2, 4)
+        load_list(3)
+        load_list(4)
+        load_gates(0, 4, 6)
+        load_list(5)
+        load_w(1)
+        load_gates(0, 6, 8)
+        load_list(6)
+        load_list(7)
         for i in range(1, BLOCKS):
-            for d in range(0, D, 2):
-                load_gates(i, d, d + 2)
-                if d == 2 and i + 1 < BLOCKS:
-                    nc.sync.dma_start(out=w_raw[i + 1][:], in_=w_view[:, :, (i + 1) * P : (i + 2) * P])
+            load_gates(i, 0, 4)
+            if i + 1 < BLOCKS:
+                load_w(i + 1)
+            load_gates(i, 4, 8)
 
         def quantize_w(i):
             nc.vector.quantize_mx(
@@ -106,7 +119,9 @@ def tile_picked_agg_lin_bias_sub_l_kernel(
         def regroup_x(c):
             n = CHUNKS[c][1]
             cut = n // 2 if c < len(CHUNKS) - 1 else n * 5 // 8
-            src = x_raw[c][:].rearrange("p j t -> p t j")
+            load = max(u for u, (t0, size) in enumerate(X_LOADS) if t0 <= CHUNKS[c][0])
+            first = CHUNKS[c][0] - X_LOADS[load][0]
+            src = x_raw[load][:, :, first : first + n].rearrange("p j t -> p t j")
             nc.scalar.copy(x_bf[c][:, cut:n, :], src[:, cut:n, :])
             nc.vector.tensor_copy(out=x_bf[c][:, 0:cut, :], in_=src[:, 0:cut, :])
 
@@ -156,12 +171,22 @@ def tile_picked_agg_lin_bias_sub_l_kernel(
             summed = D - 1 if last_block else D
             acc = [psum.tile([P, P], F32, name="acc%d" % q) for q in range(V // P)]
             for d in range(summed):
-                g = ring.tile([P, V], F32, name="g")
-                nc.vector.tensor_tensor(g[:], y[i][:].indirect(pos[d][:]), gates[i][:, d, :], MULT)
-                for q in range(V // P):
-                    nc.tensor.matmul(
-                        acc[q][:], g[:, q * P : (q + 1) * P], ident[:], start=(d == 0), stop=(d == summed - 1), is_transpose=True
+                pieces = 2 if last_block and d == summed - 1 else 1
+                n = V // pieces
+                for v0 in range(0, V, n):
+                    g = ring.tile([P, n], F32, name="g")
+                    nc.vector.tensor_tensor(
+                        g[:], y[i][:].indirect(pos[d][:, v0 // 16 : (v0 + n) // 16]), gates[i][:, d, v0 : v0 + n], MULT
                     )
+                    for q in range(n // P):
+                        nc.tensor.matmul(
+                            acc[v0 // P + q][:],
+                            g[:, q * P : (q + 1) * P],
+                            ident[:],
+                            start=(d == 0),
+                            stop=(d == summed - 1),
+                            is_transpose=True,
+                        )
                 if d == 3 and not last_block:
                     prepare_block(i + 1)
             turned = flip.tile([P, V], F32, name="turned")

@@ -9,7 +9,7 @@ PACK = 4
 BLOCKS = N // P
 CHUNK = 256
 CHUNKS = tuple((t0, CHUNK) for t0 in range(0, T, CHUNK))
-X_LOADS = ((0, 512), (512, 256), (768, 256))
+X_LOADS = CHUNKS
 TAIL = ((0, 384), (384, 128))
 
 F32 = mybir.dt.float32
@@ -40,6 +40,7 @@ def tile_picked_agg_lin_bias_sub_l_kernel(
         x_view = xT.rearrange("(p j) t -> p j t", j=PACK)
 
         ident = keep.tile([P, P], F32, name="ident")
+        b_rows = keep.tile([P, P], F32, name="b_rows")
         bias = keep.tile([P, BLOCKS], F32, name="bias")
         warm = keep.tile([P, 1], F32, name="warm")
 
@@ -61,13 +62,14 @@ def tile_picked_agg_lin_bias_sub_l_kernel(
                 in_=gate[d0:d1, i * P : (i + 1) * P, :].rearrange("d p v -> p d v"),
             )
 
+        nc.gpsimd.memset(b_rows[:], 0.0)
+        nc.sync.dma_start(out=b_rows[0:BLOCKS, :], in_=b.rearrange("(c p) o -> c (p o)", p=P))
         make_identity(nc, ident[:])
         nc.vector.memset(warm[:], 0.0)
         nc.scalar.activation(warm[:], warm[:], IDENTITY)
         nc.sync.dma_start(out=w_raw[0][:], in_=w_view[:, :, 0:P])
         for c, (t0, n) in enumerate(X_LOADS):
             nc.sync.dma_start(out=x_raw[c][:], in_=x_view[:, :, t0 : t0 + n])
-        nc.sync.dma_start(out=bias[:], in_=b.rearrange("(c p) o -> p (c o)", p=P))
         def load_list(d):
             nc.sync.dma_start(pos[d][:], lists[d])
 
@@ -112,6 +114,10 @@ def tile_picked_agg_lin_bias_sub_l_kernel(
                 start=True,
                 stop=True,
             )
+
+        b_bank = psum.tile([P, V], F32, name="back")
+        nc.tensor.transpose(b_bank[:, 0:P], b_rows[:], ident[:])
+        nc.scalar.copy(bias[:], b_bank[:, 0:BLOCKS])
 
         nc.vector.tensor_copy(out=w_bf[0][:], in_=w_raw[0][:].rearrange("p j m -> p m j"))
         quantize_w(0)

@@ -3,14 +3,26 @@ from contextlib import ExitStack
 import concourse.mybir as mybir
 from concourse.masks import make_identity
 
-K, T, D, V, N = 512, 1024, 8, 512, 512
+K = 512
+T = 1024
+N = 512
+V = 512
+D = 8
+
 P = 128
 PACK = 4
+OFFSET_ROWS = 16
 BLOCKS = N // P
-CHUNK = 256
-CHUNKS = tuple((t0, CHUNK) for t0 in range(0, T, CHUNK))
-X_LOADS = CHUNKS
-TAIL = ((0, 384), (384, 128))
+QUARTERS = V // P
+BANK = 512
+
+X_LOADS = ((0, 512), (512, 384), (896, 128))
+X_CHUNKS = ((0, 256), (256, 256), (512, 256), (768, 128), (896, 128))
+VECTOR_NODES = (128, 128, 128, 64, 80)
+
+PREPARE_AFTER = 4
+LAST_SUMMED = ((0, 256), (256, 256))
+LAST_ADDED = ((0, 384), (384, 128))
 
 F32 = mybir.dt.float32
 BF16 = mybir.dt.bfloat16
@@ -30,190 +42,187 @@ def tile_picked_agg_lin_bias_sub_l_kernel(
 ):
     nc = tc.nc
     lists = (pos1, pos2, pos3, pos4, pos5, pos6, pos7, pos8)
+
     with ExitStack() as ctx:
         keep = ctx.enter_context(tc.tile_pool(name="keep", bufs=1))
         ring = ctx.enter_context(tc.tile_pool(name="ring", bufs=6))
-        flip = ctx.enter_context(tc.tile_pool(name="flip", bufs=2))
+        ends = ctx.enter_context(tc.tile_pool(name="ends", bufs=2))
         psum = ctx.enter_context(tc.psum_pool(name="psum", bufs=1))
 
-        w_view = w.rearrange("(p j) m -> p j m", j=PACK)
-        x_view = xT.rearrange("(p j) t -> p j t", j=PACK)
-
         ident = keep.tile([P, P], F32, name="ident")
-        b_rows = keep.tile([P, P], F32, name="b_rows")
-        bias = keep.tile([P, BLOCKS], F32, name="bias")
-        warm = keep.tile([P, 1], F32, name="warm")
-
+        table_load = keep.tile([P, 1], F32, name="table_load")
+        bias_first = keep.tile([P, 1], F32, name="bias_first")
+        bias_rest = keep.tile([P, BLOCKS - 1], F32, name="bias_rest")
         w_raw = [keep.tile([P, PACK, P], F32, name="w_raw%d" % i) for i in range(BLOCKS)]
-        w_bf = [keep.tile([P, P, PACK], BF16, name="w_bf%d" % i, align_bytes=64) for i in range(BLOCKS)]
+        w_grouped = [keep.tile([P, P, PACK], BF16, name="w_grouped%d" % i, align_bytes=64) for i in range(BLOCKS)]
         w_codes = [keep.tile([P, P], U32, name="w_codes%d" % i, align_bytes=64) for i in range(BLOCKS)]
         w_scales = [keep.tile([P, P], U8, name="w_scales%d" % i, align_bytes=64) for i in range(BLOCKS)]
-        x_raw = [keep.tile([P, PACK, n], F32, name="x_raw%d" % c) for c, (t0, n) in enumerate(X_LOADS)]
-        x_bf = [keep.tile([P, n, PACK], BF16, name="x_bf%d" % c, align_bytes=64) for c, (t0, n) in enumerate(CHUNKS)]
-        x_codes = [keep.tile([P, n], U32, name="x_codes%d" % c, align_bytes=64) for c, (t0, n) in enumerate(CHUNKS)]
-        x_scales = [keep.tile([P, n], U8, name="x_scales%d" % c, align_bytes=64) for c, (t0, n) in enumerate(CHUNKS)]
-        pos = [keep.tile([P, V // 16], U16, name="pos_%d" % d) for d in range(D)]
+        x_raw = [keep.tile([P, PACK, n], F32, name="x_raw%d" % u) for u, (t0, n) in enumerate(X_LOADS)]
+        x_grouped = keep.tile([P, T, PACK], BF16, name="x_grouped", align_bytes=64)
+        x_codes = keep.tile([P, T], U32, name="x_codes", align_bytes=64)
+        x_scales = keep.tile([P, T], U8, name="x_scales", align_bytes=64)
+        offsets = [keep.tile([P, V // OFFSET_ROWS], U16, name="offsets%d" % d) for d in range(D)]
         gates = [keep.tile([P, D, V], F32, name="gates%d" % i) for i in range(BLOCKS)]
         y = [keep.tile([P, T], F32, name="y%d" % i) for i in range(BLOCKS)]
 
-        def load_gates(i, d0, d1):
-            nc.sync.dma_start(
-                out=gates[i][:, d0:d1, :],
-                in_=gate[d0:d1, i * P : (i + 1) * P, :].rearrange("d p v -> p d v"),
-            )
+        def channels(i):
+            return slice(i * P, (i + 1) * P)
 
-        nc.gpsimd.memset(b_rows[:], 0.0)
-        nc.sync.dma_start(out=b_rows[0:BLOCKS, :], in_=b.rearrange("(c p) o -> c (p o)", p=P))
-        make_identity(nc, ident[:])
-        nc.vector.memset(warm[:], 0.0)
-        nc.scalar.activation(warm[:], warm[:], IDENTITY)
-        nc.sync.dma_start(out=w_raw[0][:], in_=w_view[:, :, 0:P])
-        for c, (t0, n) in enumerate(X_LOADS):
-            nc.sync.dma_start(out=x_raw[c][:], in_=x_view[:, :, t0 : t0 + n])
-        def load_list(d):
-            nc.sync.dma_start(pos[d][:], lists[d])
+        def bias(i):
+            return bias_first[:, 0:1] if i == 0 else bias_rest[:, i - 1 : i]
+
+        def load_x(u):
+            t0, n = X_LOADS[u]
+            nc.sync.dma_start(out=x_raw[u][:], in_=xT.rearrange("(p j) t -> p j t", j=PACK)[:, :, t0 : t0 + n])
 
         def load_w(i):
-            nc.sync.dma_start(out=w_raw[i][:], in_=w_view[:, :, i * P : (i + 1) * P])
+            nc.sync.dma_start(out=w_raw[i][:], in_=w.rearrange("(p j) m -> p j m", j=PACK)[:, :, channels(i)])
 
-        load_list(0)
-        load_gates(0, 0, 1)
-        load_list(1)
-        load_gates(0, 1, 2)
+        def load_list(d):
+            nc.sync.dma_start(offsets[d][:], lists[d])
+
+        def load_gates(i, d, turns):
+            nc.sync.dma_start(
+                out=gates[i][:, d : d + turns, :], in_=gate[d : d + turns, channels(i), :].rearrange("d p v -> p d v")
+            )
+
+        make_identity(nc, ident[:])
+        nc.vector.memset(table_load[:], 0.0)
+        nc.scalar.activation(table_load[:], table_load[:], IDENTITY)
+
+        load_x(0)
+        load_w(0)
+        load_x(1)
+        load_x(2)
+        nc.sync.dma_start(out=bias_first[:], in_=b[0:P, :])
+        for d in range(2):
+            load_list(d)
+            load_gates(0, d, 1)
         load_list(2)
-        load_gates(0, 2, 4)
-        load_list(3)
-        load_list(4)
-        load_gates(0, 4, 6)
-        load_list(5)
+        load_gates(0, 2, 2)
         load_w(1)
-        load_gates(0, 6, 8)
-        load_list(6)
-        load_list(7)
+        for d in range(4, D, 2):
+            load_list(d - 1)
+            load_list(d)
+            load_gates(0, d, 2)
+        load_list(D - 1)
+        nc.sync.dma_start(out=bias_rest[:], in_=b[P:N, :].rearrange("(c p) o -> p (c o)", p=P))
         for i in range(1, BLOCKS):
-            load_gates(i, 0, 4)
-            if i + 1 < BLOCKS:
-                load_w(i + 1)
-            load_gates(i, 4, 8)
+            for d in range(0, D, 2):
+                load_gates(i, d, 2)
+                if d == 2 and i + 1 < BLOCKS:
+                    load_w(i + 1)
+
+        def regroup_x(c):
+            t0, n = X_CHUNKS[c]
+            u = max(load for load, (start, size) in enumerate(X_LOADS) if start <= t0)
+            first = t0 - X_LOADS[u][0]
+            cut = VECTOR_NODES[c]
+            rows = x_raw[u][:, :, first : first + n].rearrange("p j t -> p t j")
+            nc.scalar.copy(x_grouped[:, t0 + cut : t0 + n, :], rows[:, cut:n, :])
+            nc.vector.tensor_copy(out=x_grouped[:, t0 : t0 + cut, :], in_=rows[:, 0:cut, :])
+
+        def quantize_x(c):
+            t0, n = X_CHUNKS[c]
+            nc.vector.quantize_mx(
+                out=x_codes[:, t0 : t0 + n].bitcast(FP8X4),
+                scales=x_scales[:, t0 : t0 + n],
+                in_=x_grouped[:, t0 : t0 + n, :].rearrange("p t j -> p (t j)"),
+            )
 
         def quantize_w(i):
             nc.vector.quantize_mx(
                 out=w_codes[i][:].bitcast(FP8X4),
                 scales=w_scales[i][:],
-                in_=w_bf[i][:].rearrange("p m j -> p (m j)"),
+                in_=w_grouped[i][:].rearrange("p m j -> p (m j)"),
             )
 
-        def project(i, c, bank, col):
-            t0, n = CHUNKS[c]
+        def project(i, t0, n, psum_out):
             nc.tensor.matmul_mx(
-                out=bank[:, col : col + n],
+                out=psum_out,
                 lhsT=w_codes[i][:].bitcast(FP8X4),
                 lhsT_scale=w_scales[i][:],
-                rhs=x_codes[c][:].bitcast(FP8X4),
-                rhs_scale=x_scales[c][:],
+                rhs=x_codes[:, t0 : t0 + n].bitcast(FP8X4),
+                rhs_scale=x_scales[:, t0 : t0 + n],
                 start=True,
                 stop=True,
             )
 
-        b_bank = psum.tile([P, V], F32, name="back")
-        nc.tensor.transpose(b_bank[:, 0:P], b_rows[:], ident[:])
-        nc.scalar.copy(bias[:], b_bank[:, 0:BLOCKS])
+        def add_bias_on_scalar(i, t0, n, psum_in):
+            nc.scalar.activation(y[i][:, t0 : t0 + n], psum_in, IDENTITY, bias=bias(i))
 
-        nc.vector.tensor_copy(out=w_bf[0][:], in_=w_raw[0][:].rearrange("p j m -> p m j"))
-        quantize_w(0)
+        def add_bias_on_vector(i, t0, n, psum_in):
+            nc.vector.tensor_scalar(out=y[i][:, t0 : t0 + n], in0=psum_in, scalar1=bias(i), scalar2=None, op0=ADD)
 
-        def regroup_x(c):
-            n = CHUNKS[c][1]
-            cut = n // 2 if c < len(CHUNKS) - 1 else n * 5 // 8
-            load = max(u for u, (t0, size) in enumerate(X_LOADS) if t0 <= CHUNKS[c][0])
-            first = CHUNKS[c][0] - X_LOADS[load][0]
-            src = x_raw[load][:, :, first : first + n].rearrange("p j t -> p t j")
-            nc.scalar.copy(x_bf[c][:, cut:n, :], src[:, cut:n, :])
-            nc.vector.tensor_copy(out=x_bf[c][:, 0:cut, :], in_=src[:, 0:cut, :])
-
-        def quantize_x(c):
-            nc.vector.quantize_mx(
-                out=x_codes[c][:].bitcast(FP8X4),
-                scales=x_scales[c][:],
-                in_=x_bf[c][:].rearrange("p t j -> p (t j)"),
-            )
-
-        def add_bias(engine_is_scalar, bank, t0, n):
-            if engine_is_scalar:
-                nc.scalar.activation(y[0][:, t0 : t0 + n], bank[:, 0:n], IDENTITY, bias=bias[:, 0:1])
-            else:
-                nc.vector.tensor_scalar(
-                    out=y[0][:, t0 : t0 + n], in0=bank[:, 0:n], scalar1=bias[:, 0:1], scalar2=None, op0=ADD
-                )
-
-        head_banks = [psum.tile([P, V], F32, name=tag) for tag in ("y_bank0", "y_bank1", "y_bank2")]
+        head = [psum.tile([P, BANK], F32, name="head%d" % h) for h in range(3)]
         regroup_x(0)
         regroup_x(1)
         quantize_x(0)
-        project(0, 0, head_banks[0], 0)
-        regroup_x(2)
+        nc.vector.tensor_copy(out=w_grouped[0][:], in_=w_raw[0][:].rearrange("p j m -> p m j"))
         quantize_x(1)
-        project(0, 1, head_banks[0], CHUNK)
+        quantize_w(0)
+        project(0, 0, 256, head[0][:, 0:256])
+        project(0, 256, 256, head[0][:, 256:512])
+        regroup_x(2)
         regroup_x(3)
-        add_bias(True, head_banks[0], 0, 2 * CHUNK)
         quantize_x(2)
-        project(0, 2, head_banks[1], 0)
+        project(0, 512, 256, head[1][:, 0:256])
+        regroup_x(4)
+        add_bias_on_scalar(0, 0, 512, head[0][:])
         quantize_x(3)
-        project(0, 3, head_banks[2], 0)
-        add_bias(False, head_banks[1], 2 * CHUNK, CHUNK)
-        add_bias(False, head_banks[2], 3 * CHUNK, CHUNK)
+        project(0, 768, 128, head[1][:, 256:384])
+        quantize_x(4)
+        project(0, 896, 128, head[2][:, 0:128])
+        add_bias_on_vector(0, 512, 384, head[1][:, 0:384])
+        add_bias_on_vector(0, 896, 128, head[2][:, 0:128])
 
         def prepare_block(i):
-            nc.scalar.copy(w_bf[i][:], w_raw[i][:].rearrange("p j m -> p m j"))
+            nc.scalar.copy(w_grouped[i][:], w_raw[i][:].rearrange("p j m -> p m j"))
             quantize_w(i)
-            next_banks = [psum.tile([P, V], F32, name="y_bank%d" % h) for h in range(2)]
-            for c, (t0, n) in enumerate(CHUNKS):
-                project(i, c, next_banks[t0 // V], t0 % V)
-            for h in range(2):
-                nc.scalar.activation(y[i][:, h * V : (h + 1) * V], next_banks[h][:], IDENTITY, bias=bias[:, i : i + 1])
+            for h in range(T // BANK):
+                bank = psum.tile([P, BANK], F32, name="head%d" % h)
+                project(i, h * BANK, BANK, bank[:])
+                add_bias_on_scalar(i, h * BANK, BANK, bank[:])
+
+        def weighted_neighbours(i, d, v0, n):
+            weighted = ring.tile([P, n], F32, name="weighted")
+            picked = y[i][:].indirect(offsets[d][:, v0 // OFFSET_ROWS : (v0 + n) // OFFSET_ROWS])
+            nc.vector.tensor_tensor(weighted[:], picked, gates[i][:, d, v0 : v0 + n], MULT)
+            return weighted
 
         for i in range(BLOCKS):
             last_block = i == BLOCKS - 1
             summed = D - 1 if last_block else D
-            acc = [psum.tile([P, P], F32, name="acc%d" % q) for q in range(V // P)]
+            sums = [psum.tile([P, P], F32, name="sums%d" % q) for q in range(QUARTERS)]
             for d in range(summed):
-                pieces = 2 if last_block and d == summed - 1 else 1
-                n = V // pieces
-                for v0 in range(0, V, n):
-                    g = ring.tile([P, n], F32, name="g")
-                    nc.vector.tensor_tensor(
-                        g[:], y[i][:].indirect(pos[d][:, v0 // 16 : (v0 + n) // 16]), gates[i][:, d, v0 : v0 + n], MULT
-                    )
+                pieces = LAST_SUMMED if last_block and d == summed - 1 else ((0, V),)
+                for v0, n in pieces:
+                    weighted = weighted_neighbours(i, d, v0, n)
                     for q in range(n // P):
                         nc.tensor.matmul(
-                            acc[v0 // P + q][:],
-                            g[:, q * P : (q + 1) * P],
+                            sums[v0 // P + q][:],
+                            weighted[:, q * P : (q + 1) * P],
                             ident[:],
                             start=(d == 0),
                             stop=(d == summed - 1),
                             is_transpose=True,
                         )
-                if d == 3 and not last_block:
+                if d == PREPARE_AFTER and not last_block:
                     prepare_block(i + 1)
-            turned = flip.tile([P, V], F32, name="turned")
-            back = psum.tile([P, V], F32, name="back")
-            for q in range(V // P):
-                nc.scalar.copy(turned[:, q * P : (q + 1) * P], acc[q][:])
-                nc.tensor.transpose(back[:, q * P : (q + 1) * P], turned[:, q * P : (q + 1) * P], ident[:])
-            result = flip.tile([P, V], F32, name="result")
+
+            turned = psum.tile([P, V], F32, name="turned")
+            staged = ends.tile([P, V], F32, name="staged")
+            result = ends.tile([P, V], F32, name="result")
+            for q in range(QUARTERS):
+                square = slice(q * P, (q + 1) * P)
+                nc.scalar.copy(staged[:, square], sums[q][:])
+                nc.tensor.transpose(turned[:, square], staged[:, square], ident[:])
             if not last_block:
-                nc.scalar.copy(result[:], back[:])
-                nc.scalar.dma_start(out=out[i * P : (i + 1) * P, :], in_=result[:])
+                nc.scalar.copy(result[:], turned[:])
+                nc.scalar.dma_start(out=out[channels(i), :], in_=result[:])
             else:
-                tail = [ring.tile([P, n], F32, name="tail%d" % h) for h, (v0, n) in enumerate(TAIL)]
-                for h, (v0, n) in enumerate(TAIL):
-                    nc.vector.tensor_tensor(
-                        tail[h][:],
-                        y[i][:].indirect(pos[D - 1][:, v0 // 16 : (v0 + n) // 16]),
-                        gates[i][:, D - 1, v0 : v0 + n],
-                        MULT,
-                    )
-                for h, (v0, n) in enumerate(TAIL):
-                    cols = slice(v0, v0 + n)
-                    nc.vector.tensor_tensor(result[:, cols], back[:, cols], tail[h][:], ADD)
-                    nc.sync.dma_start(out=out[i * P : (i + 1) * P, cols], in_=result[:, cols])
+                added = [weighted_neighbours(i, D - 1, v0, n) for v0, n in LAST_ADDED]
+                for (v0, n), weighted in zip(LAST_ADDED, added):
+                    targets = slice(v0, v0 + n)
+                    nc.vector.tensor_tensor(result[:, targets], turned[:, targets], weighted[:], ADD)
+                    nc.sync.dma_start(out=out[channels(i), targets], in_=result[:, targets])

from contextlib import ExitStack

import concourse.mybir as mybir
from concourse.masks import make_identity

K = 512
T = 1024
N = 512
V = 512
D = 8

P = 128
PACK = 4
OFFSET_ROWS = 16
BLOCKS = N // P
QUARTERS = V // P
BANK = 512

X_LOADS = ((0, 512), (512, 384), (896, 128))
X_CHUNKS = ((0, 256), (256, 256), (512, 256), (768, 128), (896, 128))
VECTOR_NODES = (128, 128, 128, 64, 80)

PREPARE_AFTER = 4
LAST_SUMMED = ((0, 256), (256, 256))
LAST_ADDED = ((0, 384), (384, 128))

F32 = mybir.dt.float32
BF16 = mybir.dt.bfloat16
U32 = mybir.dt.uint32
U16 = mybir.dt.uint16
U8 = mybir.dt.uint8
FP8X4 = mybir.dt.float8_e4m3fn_x4
MULT = mybir.AluOpType.mult
ADD = mybir.AluOpType.add
IDENTITY = mybir.ActivationFunctionType.Identity

FLOPS = 2 * K * N * T + 2 * D * N * V


def tile_picked_agg_lin_bias_sub_l_kernel(
    tc, xT, w, b, gate, pos1, pos2, pos3, pos4, pos5, pos6, pos7, pos8, out
):
    nc = tc.nc
    lists = (pos1, pos2, pos3, pos4, pos5, pos6, pos7, pos8)

    with ExitStack() as ctx:
        keep = ctx.enter_context(tc.tile_pool(name="keep", bufs=1))
        ring = ctx.enter_context(tc.tile_pool(name="ring", bufs=6))
        ends = ctx.enter_context(tc.tile_pool(name="ends", bufs=2))
        psum = ctx.enter_context(tc.psum_pool(name="psum", bufs=1))

        ident = keep.tile([P, P], F32, name="ident")
        table_load = keep.tile([P, 1], F32, name="table_load")
        bias_first = keep.tile([P, 1], F32, name="bias_first")
        bias_rest = keep.tile([P, BLOCKS - 1], F32, name="bias_rest")
        w_raw = [keep.tile([P, PACK, P], F32, name="w_raw%d" % i) for i in range(BLOCKS)]
        w_grouped = [keep.tile([P, P, PACK], BF16, name="w_grouped%d" % i, align_bytes=64) for i in range(BLOCKS)]
        w_codes = [keep.tile([P, P], U32, name="w_codes%d" % i, align_bytes=64) for i in range(BLOCKS)]
        w_scales = [keep.tile([P, P], U8, name="w_scales%d" % i, align_bytes=64) for i in range(BLOCKS)]
        x_raw = [keep.tile([P, PACK, n], F32, name="x_raw%d" % u) for u, (t0, n) in enumerate(X_LOADS)]
        x_grouped = keep.tile([P, T, PACK], BF16, name="x_grouped", align_bytes=64)
        x_codes = keep.tile([P, T], U32, name="x_codes", align_bytes=64)
        x_scales = keep.tile([P, T], U8, name="x_scales", align_bytes=64)
        offsets = [keep.tile([P, V // OFFSET_ROWS], U16, name="offsets%d" % d) for d in range(D)]
        gates = [keep.tile([P, D, V], F32, name="gates%d" % i) for i in range(BLOCKS)]
        y = [keep.tile([P, T], F32, name="y%d" % i) for i in range(BLOCKS)]

        def channels(i):
            return slice(i * P, (i + 1) * P)

        def bias(i):
            return bias_first[:, 0:1] if i == 0 else bias_rest[:, i - 1 : i]

        def load_x(u):
            t0, n = X_LOADS[u]
            nc.sync.dma_start(out=x_raw[u][:], in_=xT.rearrange("(p j) t -> p j t", j=PACK)[:, :, t0 : t0 + n])

        def load_w(i):
            nc.sync.dma_start(out=w_raw[i][:], in_=w.rearrange("(p j) m -> p j m", j=PACK)[:, :, channels(i)])

        def load_list(d):
            nc.sync.dma_start(offsets[d][:], lists[d])

        def load_gates(i, d, turns):
            nc.sync.dma_start(
                out=gates[i][:, d : d + turns, :], in_=gate[d : d + turns, channels(i), :].rearrange("d p v -> p d v")
            )

        make_identity(nc, ident[:])
        nc.vector.memset(table_load[:], 0.0)
        nc.scalar.activation(table_load[:], table_load[:], IDENTITY)

        load_x(0)
        load_w(0)
        load_x(1)
        load_x(2)
        nc.sync.dma_start(out=bias_first[:], in_=b[0:P, :])
        for d in range(2):
            load_list(d)
            load_gates(0, d, 1)
        load_list(2)
        load_gates(0, 2, 2)
        load_w(1)
        for d in range(4, D, 2):
            load_list(d - 1)
            load_list(d)
            load_gates(0, d, 2)
        load_list(D - 1)
        nc.sync.dma_start(out=bias_rest[:], in_=b[P:N, :].rearrange("(c p) o -> p (c o)", p=P))
        for i in range(1, BLOCKS):
            for d in range(0, D, 2):
                load_gates(i, d, 2)
                if d == 2 and i + 1 < BLOCKS:
                    load_w(i + 1)

        def regroup_x(c):
            t0, n = X_CHUNKS[c]
            u = max(load for load, (start, size) in enumerate(X_LOADS) if start <= t0)
            first = t0 - X_LOADS[u][0]
            cut = VECTOR_NODES[c]
            rows = x_raw[u][:, :, first : first + n].rearrange("p j t -> p t j")
            nc.scalar.copy(x_grouped[:, t0 + cut : t0 + n, :], rows[:, cut:n, :])
            nc.vector.tensor_copy(out=x_grouped[:, t0 : t0 + cut, :], in_=rows[:, 0:cut, :])

        def quantize_x(c):
            t0, n = X_CHUNKS[c]
            nc.vector.quantize_mx(
                out=x_codes[:, t0 : t0 + n].bitcast(FP8X4),
                scales=x_scales[:, t0 : t0 + n],
                in_=x_grouped[:, t0 : t0 + n, :].rearrange("p t j -> p (t j)"),
            )

        def quantize_w(i):
            nc.vector.quantize_mx(
                out=w_codes[i][:].bitcast(FP8X4),
                scales=w_scales[i][:],
                in_=w_grouped[i][:].rearrange("p m j -> p (m j)"),
            )

        def project(i, t0, n, psum_out):
            nc.tensor.matmul_mx(
                out=psum_out,
                lhsT=w_codes[i][:].bitcast(FP8X4),
                lhsT_scale=w_scales[i][:],
                rhs=x_codes[:, t0 : t0 + n].bitcast(FP8X4),
                rhs_scale=x_scales[:, t0 : t0 + n],
                start=True,
                stop=True,
            )

        def add_bias_on_scalar(i, t0, n, psum_in):
            nc.scalar.activation(y[i][:, t0 : t0 + n], psum_in, IDENTITY, bias=bias(i))

        def add_bias_on_vector(i, t0, n, psum_in):
            nc.vector.tensor_scalar(out=y[i][:, t0 : t0 + n], in0=psum_in, scalar1=bias(i), scalar2=None, op0=ADD)

        head = [psum.tile([P, BANK], F32, name="head%d" % h) for h in range(3)]
        regroup_x(0)
        regroup_x(1)
        quantize_x(0)
        nc.vector.tensor_copy(out=w_grouped[0][:], in_=w_raw[0][:].rearrange("p j m -> p m j"))
        quantize_x(1)
        quantize_w(0)
        project(0, 0, 256, head[0][:, 0:256])
        project(0, 256, 256, head[0][:, 256:512])
        regroup_x(2)
        regroup_x(3)
        quantize_x(2)
        project(0, 512, 256, head[1][:, 0:256])
        regroup_x(4)
        add_bias_on_scalar(0, 0, 512, head[0][:])
        quantize_x(3)
        project(0, 768, 128, head[1][:, 256:384])
        quantize_x(4)
        project(0, 896, 128, head[2][:, 0:128])
        add_bias_on_vector(0, 512, 384, head[1][:, 0:384])
        add_bias_on_vector(0, 896, 128, head[2][:, 0:128])

        def prepare_block(i):
            nc.scalar.copy(w_grouped[i][:], w_raw[i][:].rearrange("p j m -> p m j"))
            quantize_w(i)
            for h in range(T // BANK):
                bank = psum.tile([P, BANK], F32, name="head%d" % h)
                project(i, h * BANK, BANK, bank[:])
                add_bias_on_scalar(i, h * BANK, BANK, bank[:])

        def weighted_neighbours(i, d, v0, n):
            weighted = ring.tile([P, n], F32, name="weighted")
            picked = y[i][:].indirect(offsets[d][:, v0 // OFFSET_ROWS : (v0 + n) // OFFSET_ROWS])
            nc.vector.tensor_tensor(weighted[:], picked, gates[i][:, d, v0 : v0 + n], MULT)
            return weighted

        for i in range(BLOCKS):
            last_block = i == BLOCKS - 1
            summed = D - 1 if last_block else D
            sums = [psum.tile([P, P], F32, name="sums%d" % q) for q in range(QUARTERS)]
            for d in range(summed):
                pieces = LAST_SUMMED if last_block and d == summed - 1 else ((0, V),)
                for v0, n in pieces:
                    weighted = weighted_neighbours(i, d, v0, n)
                    for q in range(n // P):
                        nc.tensor.matmul(
                            sums[v0 // P + q][:],
                            weighted[:, q * P : (q + 1) * P],
                            ident[:],
                            start=(d == 0),
                            stop=(d == summed - 1),
                            is_transpose=True,
                        )
                if d == PREPARE_AFTER and not last_block:
                    prepare_block(i + 1)

            turned = psum.tile([P, V], F32, name="turned")
            staged = ends.tile([P, V], F32, name="staged")
            result = ends.tile([P, V], F32, name="result")
            for q in range(QUARTERS):
                square = slice(q * P, (q + 1) * P)
                nc.scalar.copy(staged[:, square], sums[q][:])
                nc.tensor.transpose(turned[:, square], staged[:, square], ident[:])
            if not last_block:
                nc.scalar.copy(result[:], turned[:])
                nc.scalar.dma_start(out=out[channels(i), :], in_=result[:])
            else:
                added = [weighted_neighbours(i, D - 1, v0, n) for v0, n in LAST_ADDED]
                for (v0, n), weighted in zip(LAST_ADDED, added):
                    targets = slice(v0, v0 + n)
                    nc.vector.tensor_tensor(result[:, targets], turned[:, targets], weighted[:], ADD)
                    nc.sync.dma_start(out=out[channels(i), targets], in_=result[:, targets])
